import numpy as np
import ml_dtypes


def mxq(x, axis, fmt="e4m3"):
    dtype, down = {"e4m3": (ml_dtypes.float8_e4m3fn, 7), "e5m2": (ml_dtypes.float8_e5m2, 14)}[fmt]
    v = np.moveaxis(np.asarray(x, np.float32).astype(ml_dtypes.bfloat16).astype(np.float64), axis, -1)
    blocks = v.reshape(v.shape[:-1] + (-1, 32))
    amax = np.abs(blocks).max(-1, keepdims=True)
    byte = np.maximum(np.where(amax > 0, np.frexp(amax)[1] - 1 + 127, 0) - down, 1)
    scale = np.exp2(byte - 127.0)
    codes = (blocks / scale).astype(np.float32).astype(dtype).astype(np.float64)
    return np.moveaxis((codes * scale).reshape(v.shape), -1, axis)


WIDE = False


def mx_kscale(k):
    if not WIDE:
        return np.ones(k)
    levels = np.array([10, -10, 5, -5, 0])
    if k % 512:
        return np.exp2(np.random.permutation(np.resize(levels, k // 32))).repeat(32)
    a = np.empty((k // 512, 16))
    for p in range(k // 512):
        a[p, :8] = np.random.permutation(np.resize(levels, 8))
        for g in range(8):
            far = levels[np.abs(levels - a[p, g]) >= 10]
            a[p, g + 8] = far[np.random.randint(len(far))]
    return np.exp2(a.ravel()).repeat(32)


def f64(x):
    return np.asarray(x).astype(np.float64)


def striped(idx):
    return np.tile(np.asarray(idx).reshape(-1, 16).T, (8, 1)).astype(np.uint16)


def unstriped(offs):
    return offs[:16].T.reshape(-1).astype(np.int64)


E2M1 = np.array([0.0, 0.5, 1.0, 1.5, 2.0, 3.0, 4.0, 6.0, -0.0, -0.5, -1.0, -1.5, -2.0, -3.0, -4.0, -6.0])


def pack_weight(w, fmt):
    k, n = w.shape
    w = f64(np.asarray(w, np.float32).astype(ml_dtypes.bfloat16)).reshape(k // 32, 32, n)
    amax = np.abs(w).max(1)
    if fmt == "e4m3":
        byte = np.frexp(amax)[1] - 1 + 127 - 7
    else:
        mant, ex = np.frexp(amax / 6.0)
        byte = np.where(mant > 0.5, ex, ex - 1) + 127
    byte = np.clip(np.where(amax > 0, byte, 1), 1, 254)
    scaled = (w * np.exp2(127.0 - byte)[:, None, :]).reshape(k, n).astype(np.float32)
    by_word = np.ascontiguousarray(scaled.reshape(k // 512, 128, 4, n).transpose(0, 1, 3, 2))
    if fmt == "e4m3":
        words = by_word.astype(ml_dtypes.float8_e4m3fn).view(np.uint8)
    else:
        c = by_word.astype(ml_dtypes.float4_e2m1fn).view(np.uint8) & 0xF
        words = (c[..., 0::2] | (c[..., 1::2] << 4)).reshape(k // 512, 128, 2 * n)
    return np.ascontiguousarray(words), np.ascontiguousarray(byte.astype(np.uint8).reshape(k // 512, 16, n))


def unpack_weight(words, scales, fmt):
    g, _, n = scales.shape
    words = np.ascontiguousarray(words).reshape(g, 128, n, -1)
    if fmt == "e4m3":
        vals = words.view(ml_dtypes.float8_e4m3fn).astype(np.float64)
    else:
        nib = np.empty((g, 128, n, 4), np.uint8)
        nib[..., 0::2] = words & 0xF
        nib[..., 1::2] = words >> 4
        vals = E2M1[nib]
    vals = vals * np.repeat(np.exp2(scales.astype(np.float64) - 127.0), 8, axis=1)[..., None]
    return vals.transpose(0, 1, 3, 2).reshape(g * 512, n)


def e4m3fn_bytes(y):
    return np.clip(np.asarray(y, np.float64), -448.0, 448.0).astype(np.float32).astype(ml_dtypes.float8_e4m3fn).view(np.uint8)


def e4m3fn_values(b):
    return np.asarray(b, np.uint8).view(ml_dtypes.float8_e4m3fn).astype(np.float64)


K, V, J, N, E = 512, 1024, 256, 256, 512


def setup_inputs():
    n = np.random.standard_normal
    idx = np.random.permutation(V)[:J]
    idx2 = np.random.permutation(V)[:J]
    idx3 = np.random.permutation(E)[:J]
    fk = mx_kscale(K)
    wp = pack_weight(n((K, N)) * 1 / np.sqrt(K) / fk[:, None], "e4m3")
    w2p = pack_weight(n((K, N)) * 1 / np.sqrt(K) / fk[:, None], "e2m1")
    return {
        "ca": e4m3fn_bytes(60.0 * n((K, V))),
        "sa": (np.random.uniform(0.004, 0.012, (K, 1)) * fk[:, None]).astype(np.float32),
        "sb": (np.random.uniform(0.004, 0.012, (K, 1)) * fk[:, None]).astype(np.float32),
        "w_words": wp[0],
        "w_scales": wp[1],
        "w2_words": w2p[0],
        "w2_scales": w2p[1],
        "so": (np.random.uniform(0.5, 1.6, (N, 1))).astype(np.float32),
        "offs": striped(idx),
        "offs2": striped(idx2),
        "offs3": striped(idx3),
    }


def reference(ca, sa, sb, w_words, w_scales, w2_words, w2_scales, so, offs, offs2, offs3):
    idx = unstriped(offs)
    idx2 = unstriped(offs2)
    idx3 = unstriped(offs3)
    wu = unpack_weight(w_words, w_scales, "e4m3")
    w2u = unpack_weight(w2_words, w2_scales, "e2m1")
    z1 = np.maximum(e4m3fn_values(ca)[:, idx], e4m3fn_values(ca)[:, idx2]) * f64(sa)
    z2 = np.minimum(e4m3fn_values(ca)[:, idx], e4m3fn_values(ca)[:, idx2]) * f64(sb)
    z1q = mxq(z1, 0, "e4m3")
    z2q = mxq(z2, 0, "e4m3")
    p = wu.T @ z1q + w2u.T @ z2q
    y = np.zeros((N, E))
    y[:, idx3] = p * f64(so)
    return y

@@ -1,0 +1,121 @@
+from contextlib import ExitStack
+
+import concourse.mybir as mybir
+
+K, V, J, N, E = 512, 1024, 256, 256, 512
+FLOPS = 2 * 2 * K * N * J
+
+F32 = mybir.dt.float32
+BF16 = mybir.dt.bfloat16
+I32 = mybir.dt.int32
+U32 = mybir.dt.uint32
+U16 = mybir.dt.uint16
+U8 = mybir.dt.uint8
+FP8 = mybir.dt.float8_e4m3fn
+FP8X4 = mybir.dt.float8_e4m3fn_x4
+FP4X4 = mybir.dt.float4_e2m1fn_x4
+ALU = mybir.AluOpType
+COPY = mybir.ActivationFunctionType.Copy
+
+P = 128
+PACK = 4
+HALF = J // 2
+LINE = 4
+
+
+def tile_list_sortedpair_kernel(tc, ca, sa, sb, w_words, w_scales, w2_words, w2_scales, so, offs, offs2, offs3, out):
+    nc = tc.nc
+    with ExitStack() as ctx:
+        keep = ctx.enter_context(tc.tile_pool(name="keep", bufs=1))
+        psum = ctx.enter_context(tc.psum_pool(name="psum", bufs=1))
+
+        table = [keep.tile([P, V], U8, name=f"table{t}") for t in range(PACK)]
+        list_a = keep.tile([P, J // 16], U16, name="list_a")
+        list_b = keep.tile([P, J // 16], U16, name="list_b")
+        list_out = keep.tile([P, J // 16], U16, name="list_out")
+        step_hi = keep.tile([P, PACK], F32, name="step_hi")
+        step_lo = keep.tile([P, PACK], F32, name="step_lo")
+        gain = keep.tile([P, N // P], F32, name="gain")
+        w_codes = keep.tile([P, N], U32, name="w_codes", align_bytes=64)
+        w2_codes = keep.tile([P, 2 * N], U8, name="w2_codes", align_bytes=64)
+        w_plane = keep.tile([P, 2 * N], U8, name="w_plane", align_bytes=64)
+        pages = [keep.tile([P, E], F32, name=f"page{b}") for b in range(N // P)]
+
+        nc.vector.memset(w_plane[:].bitcast(I32), 0)
+        for page in pages:
+            nc.gpsimd.memset(page[:], 0.0)
+
+        rows = ca.rearrange("(p t) v -> p t v", t=PACK)
+        nc.sync.dma_start(out=table[0][:], in_=rows[:, 0, :])
+        nc.sync.dma_start(list_a[:], offs)
+        nc.sync.dma_start(list_b[:], offs2)
+        for t in range(1, PACK):
+            nc.sync.dma_start(out=table[t][:], in_=rows[:, t, :])
+        nc.scalar.dma_start(out=step_hi[:], in_=sa.rearrange("(p t) o -> p (t o)", t=PACK))
+        nc.scalar.dma_start(out=step_lo[:], in_=sb.rearrange("(p t) o -> p (t o)", t=PACK))
+        nc.sync.dma_start(out=w_codes[:].bitcast(I32), in_=w_words[0].rearrange("p n t -> p (n t)").bitcast(I32))
+        nc.sync.dma_start(out=w2_codes[:].bitcast(I32), in_=w2_words[0].bitcast(I32))
+        for q in range(4):
+            nc.sync.dma_start(out=w_plane[32 * q : 32 * q + 4, 0:N].bitcast(I32), in_=w_scales[0, 4 * q : 4 * q + 4, :].bitcast(I32))
+            nc.sync.dma_start(out=w_plane[32 * q : 32 * q + 4, N : 2 * N].bitcast(I32), in_=w2_scales[0, 4 * q : 4 * q + 4, :].bitcast(I32))
+        nc.sync.dma_start(list_out[:], offs3)
+        with nc.allow_non_contiguous_dma(reason="one float32 a partition for each block of 128 output features"):
+            nc.sync.dma_start(out=gain[:], in_=so.rearrange("(b p) o -> p (b o)", p=P))
+
+        val_a = keep.tile([P, PACK, J], F32, name="val_a")
+        val_b = keep.tile([P, PACK, J], F32, name="val_b")
+        for t in range(PACK):
+            for name, offsets, val in (("a", list_a, val_a), ("b", list_b, val_b)):
+                picked = keep.tile([P, J], U8, name=f"picked_{name}{t}")
+                nc.vector.tensor_copy(picked[:], table[t][:].indirect(offsets[:]))
+                nc.scalar.copy(val[:, t, :], picked[:].bitcast(FP8))
+
+        for h in range(2):
+            cols = slice(h * HALF, (h + 1) * HALF)
+            grouped = keep.tile([P, 2, HALF * PACK], BF16, name=f"grouped{h}", align_bytes=64)
+            ordered = [keep.tile([P, PACK, HALF], F32, name=f"ordered{h}_{s}") for s in range(2)]
+            for s, op in enumerate((ALU.max, ALU.min)):
+                nc.vector.tensor_tensor(ordered[s][:], val_a[:, :, cols], val_b[:, :, cols], op)
+            for s, step in enumerate((step_hi, step_lo)):
+                nc.vector.tensor_tensor(
+                    grouped[:, s, :].rearrange("p (c i t) -> p c t i", i=LINE, t=PACK),
+                    ordered[s][:].rearrange("p t (c i) -> p c t i", i=LINE),
+                    step[:].rearrange("p (a t b) -> p a t b", a=1, b=1).to_broadcast([P, HALF // LINE, PACK, LINE]),
+                    ALU.mult,
+                )
+            codes = keep.tile([P, 2 * HALF], U32, name=f"codes{h}", align_bytes=64)
+            plane = keep.tile([P, 2 * HALF], U8, name=f"plane{h}", align_bytes=64)
+            nc.vector.quantize_mx(out=codes[:].bitcast(FP8X4), scales=plane[:], in_=grouped[:].rearrange("p s x -> p (s x)"))
+            for b in range(N // P):
+                acc = psum.tile([P, HALF], F32, name=f"acc{h}_{b}")
+                nc.tensor.matmul_mx(
+                    out=acc[:],
+                    lhsT=w_codes[:, b * P : (b + 1) * P].bitcast(FP8X4),
+                    lhsT_scale=w_plane[:, b * P : (b + 1) * P],
+                    rhs=codes[:, 0:HALF].bitcast(FP8X4),
+                    rhs_scale=plane[:, 0:HALF],
+                    start=True,
+                    stop=False,
+                )
+                nc.tensor.matmul_mx(
+                    out=acc[:],
+                    lhsT=w2_codes[:, 2 * b * P : 2 * (b + 1) * P].bitcast(FP4X4),
+                    lhsT_scale=w_plane[:, N + b * P : N + (b + 1) * P],
+                    rhs=codes[:, HALF : 2 * HALF].bitcast(FP8X4),
+                    rhs_scale=plane[:, HALF : 2 * HALF],
+                    start=False,
+                    stop=True,
+                )
+                sums = keep.tile([P, HALF], F32, name=f"sums{h}_{b}")
+                if h == 0:
+                    nc.scalar.copy(sums[:], acc[:])
+                else:
+                    nc.vector.tensor_copy(sums[:], acc[:])
+                nc.scalar.activation(
+                    out=pages[b][:].indirect(list_out[:, h * HALF // 16 : (h + 1) * HALF // 16]),
+                    in_=sums[:],
+                    func=COPY,
+                    scale=gain[:, b : b + 1],
+                )
+        nc.sync.dma_start(out=out[0:P, :], in_=pages[0][:])
+        nc.scalar.dma_start(out=out[P : 2 * P, :], in_=pages[1][:])

@@ -27,6 +27,7 @@ def tile_list_sortedpair_kernel(tc, ca, sa, sb, w_words, w_scales, w2_words, w2_
     nc = tc.nc
     with ExitStack() as ctx:
         keep = ctx.enter_context(tc.tile_pool(name="keep", bufs=1))
+        ring = ctx.enter_context(tc.tile_pool(name="ring", bufs=3))
         psum = ctx.enter_context(tc.psum_pool(name="psum", bufs=1))
 
         table = [keep.tile([P, V], U8, name=f"table{t}") for t in range(PACK)]
@@ -64,58 +65,85 @@ def tile_list_sortedpair_kernel(tc, ca, sa, sb, w_words, w_scales, w2_words, w2_
 
         val_a = keep.tile([P, PACK, J], F32, name="val_a")
         val_b = keep.tile([P, PACK, J], F32, name="val_b")
-        for t in range(PACK):
-            for name, offsets, val in (("a", list_a, val_a), ("b", list_b, val_b)):
-                picked = keep.tile([P, J], U8, name=f"picked_{name}{t}")
+        low = keep.tile([P, PACK, J], F32, name="low")
+        high_rows = [keep.tile([P, PACK * HALF], F32, name=f"high{h}", align_bytes=64) for h in range(2)]
+        high = [rows_h[:].rearrange("p (t j) -> p t j", t=PACK) for rows_h in high_rows]
+        z_lo1 = keep.tile([P, HALF * PACK], BF16, name="z_lo1", align_bytes=64)
+        z_hi0 = keep.tile([P, HALF * PACK], BF16, name="z_hi0", align_bytes=64)
+        z_hi = [z_hi0, z_lo1]
+        z_lo = [high_rows[1][:, 0 : 2 * HALF].bitcast(BF16), z_lo1[:]]
+        cols = [slice(h * HALF, (h + 1) * HALF) for h in range(2)]
+        acc = [[psum.tile([P, HALF], F32, name=f"acc{h}_{b}") for b in range(N // P)] for h in range(2)]
+
+        def look_up(t):
+            for offsets, val in ((list_a, val_a), (list_b, val_b)):
+                picked = ring.tile([P, J], U8, name="picked")
                 nc.vector.tensor_copy(picked[:], table[t][:].indirect(offsets[:]))
                 nc.scalar.copy(val[:, t, :], picked[:].bitcast(FP8))
 
-        for h in range(2):
-            cols = slice(h * HALF, (h + 1) * HALF)
-            grouped = keep.tile([P, 2, HALF * PACK], BF16, name=f"grouped{h}", align_bytes=64)
-            ordered = [keep.tile([P, PACK, HALF], F32, name=f"ordered{h}_{s}") for s in range(2)]
-            for s, op in enumerate((ALU.max, ALU.min)):
-                nc.vector.tensor_tensor(ordered[s][:], val_a[:, :, cols], val_b[:, :, cols], op)
-            for s, step in enumerate((step_hi, step_lo)):
-                nc.vector.tensor_tensor(
-                    grouped[:, s, :].rearrange("p (c i t) -> p c t i", i=LINE, t=PACK),
-                    ordered[s][:].rearrange("p t (c i) -> p c t i", i=LINE),
-                    step[:].rearrange("p (a t b) -> p a t b", a=1, b=1).to_broadcast([P, HALF // LINE, PACK, LINE]),
-                    ALU.mult,
-                )
-            codes = keep.tile([P, 2 * HALF], U32, name=f"codes{h}", align_bytes=64)
-            plane = keep.tile([P, 2 * HALF], U8, name=f"plane{h}", align_bytes=64)
-            nc.vector.quantize_mx(out=codes[:].bitcast(FP8X4), scales=plane[:], in_=grouped[:].rearrange("p s x -> p (s x)"))
+        def lower(t):
+            nc.vector.tensor_tensor(low[:, t, :], val_a[:, t, :], val_b[:, t, :], ALU.min)
+            for h in range(2):
+                nc.scalar.activation(out=z_lo[h][:, t :: PACK], in_=low[:, t, cols[h]], func=COPY, scale=step_lo[:, t : t + 1])
+
+        def upper(h, slots):
+            nc.vector.tensor_tensor(high[h][:, slots, :], val_a[:, slots, cols[h]], val_b[:, slots, cols[h]], ALU.max)
+
+        def scale_upper(h):
+            nc.vector.tensor_tensor(
+                z_hi[h][:].rearrange("p (c i t) -> p c t i", i=LINE, t=PACK),
+                high[h].rearrange("p t (c i) -> p c t i", i=LINE),
+                step_hi[:].rearrange("p (a t b) -> p a t b", a=1, b=1).to_broadcast([P, HALF // LINE, PACK, LINE]),
+                ALU.mult,
+            )
+
+        def product(h, z, name, weights, first):
+            codes = keep.tile([P, HALF], U32, name=f"codes_{name}{h}", align_bytes=64)
+            plane = keep.tile([P, HALF], U8, name=f"plane_{name}{h}", align_bytes=64)
+            nc.vector.quantize_mx(out=codes[:].bitcast(FP8X4), scales=plane[:], in_=z)
             for b in range(N // P):
-                acc = psum.tile([P, HALF], F32, name=f"acc{h}_{b}")
+                lhs, lhs_plane = weights(b)
                 nc.tensor.matmul_mx(
-                    out=acc[:],
-                    lhsT=w_codes[:, b * P : (b + 1) * P].bitcast(FP8X4),
-                    lhsT_scale=w_plane[:, b * P : (b + 1) * P],
-                    rhs=codes[:, 0:HALF].bitcast(FP8X4),
-                    rhs_scale=plane[:, 0:HALF],
-                    start=True,
-                    stop=False,
+                    out=acc[h][b][:], lhsT=lhs, lhsT_scale=lhs_plane, rhs=codes[:].bitcast(FP8X4), rhs_scale=plane[:], start=first, stop=not first
                 )
-                nc.tensor.matmul_mx(
-                    out=acc[:],
-                    lhsT=w2_codes[:, 2 * b * P : 2 * (b + 1) * P].bitcast(FP4X4),
-                    lhsT_scale=w_plane[:, N + b * P : N + (b + 1) * P],
-                    rhs=codes[:, HALF : 2 * HALF].bitcast(FP8X4),
-                    rhs_scale=plane[:, HALF : 2 * HALF],
-                    start=False,
-                    stop=True,
-                )
-                sums = keep.tile([P, HALF], F32, name=f"sums{h}_{b}")
-                if h == 0:
-                    nc.scalar.copy(sums[:], acc[:])
-                else:
-                    nc.vector.tensor_copy(sums[:], acc[:])
+
+        def w_upper(b):
+            return w_codes[:, b * P : (b + 1) * P].bitcast(FP8X4), w_plane[:, b * P : (b + 1) * P]
+
+        def w_lower(b):
+            return w2_codes[:, 2 * b * P : 2 * (b + 1) * P].bitcast(FP4X4), w_plane[:, N + b * P : N + (b + 1) * P]
+
+        def put(h, copy):
+            sums = [keep.tile([P, HALF], F32, name=f"sums{h}_{b}") for b in range(N // P)]
+            for b in range(N // P):
+                copy(sums[b][:], acc[h][b][:])
+            for b in range(N // P):
                 nc.scalar.activation(
                     out=pages[b][:].indirect(list_out[:, h * HALF // 16 : (h + 1) * HALF // 16]),
-                    in_=sums[:],
+                    in_=sums[b][:],
                     func=COPY,
                     scale=gain[:, b : b + 1],
                 )
+
+        look_up(0)
+        look_up(1)
+        lower(0)
+        look_up(2)
+        lower(1)
+        look_up(3)
+        lower(2)
+        upper(0, slice(0, PACK - 1))
+        upper(0, slice(PACK - 1, PACK))
+        lower(3)
+        scale_upper(0)
+        upper(1, slice(2, PACK))
+        product(0, z_hi[0][:], "hi", w_upper, True)
+        product(0, z_lo[0], "lo", w_lower, False)
+        upper(1, slice(0, 2))
+        product(1, z_lo[1], "lo", w_lower, True)
+        scale_upper(1)
+        put(0, nc.scalar.copy)
+        product(1, z_hi[1][:], "hi", w_upper, False)
+        put(1, nc.vector.tensor_copy)
         nc.sync.dma_start(out=out[0:P, :], in_=pages[0][:])
         nc.scalar.dma_start(out=out[P : 2 * P, :], in_=pages[1][:])

@@ -52,8 +52,8 @@ def tile_list_sortedpair_kernel(tc, ca, sa, sb, w_words, w_scales, w2_words, w2_
         nc.sync.dma_start(list_b[:], offs2)
         for t in range(1, PACK):
             nc.sync.dma_start(out=table[t][:], in_=rows[:, t, :])
-        nc.scalar.dma_start(out=step_hi[:], in_=sa.rearrange("(p t) o -> p (t o)", t=PACK))
-        nc.scalar.dma_start(out=step_lo[:], in_=sb.rearrange("(p t) o -> p (t o)", t=PACK))
+        nc.sync.dma_start(out=step_lo[:], in_=sb.rearrange("(p t) o -> p (t o)", t=PACK))
+        nc.sync.dma_start(out=step_hi[:], in_=sa.rearrange("(p t) o -> p (t o)", t=PACK))
         nc.sync.dma_start(out=w_codes[:].bitcast(I32), in_=w_words[0].rearrange("p n t -> p (n t)").bitcast(I32))
         nc.sync.dma_start(out=w2_codes[:].bitcast(I32), in_=w2_words[0].bitcast(I32))
         for q in range(4):
@@ -66,84 +66,117 @@ def tile_list_sortedpair_kernel(tc, ca, sa, sb, w_words, w_scales, w2_words, w2_
         val_a = keep.tile([P, PACK, J], F32, name="val_a")
         val_b = keep.tile([P, PACK, J], F32, name="val_b")
         low = keep.tile([P, PACK, J], F32, name="low")
-        high_rows = [keep.tile([P, PACK * HALF], F32, name=f"high{h}", align_bytes=64) for h in range(2)]
-        high = [rows_h[:].rearrange("p (t j) -> p t j", t=PACK) for rows_h in high_rows]
-        z_lo1 = keep.tile([P, HALF * PACK], BF16, name="z_lo1", align_bytes=64)
-        z_hi0 = keep.tile([P, HALF * PACK], BF16, name="z_hi0", align_bytes=64)
-        z_hi = [z_hi0, z_lo1]
-        z_lo = [high_rows[1][:, 0 : 2 * HALF].bitcast(BF16), z_lo1[:]]
+        high = [keep.tile([P, PACK, HALF], F32, name=f"high{h}") for h in range(2)]
+        z_hi = [keep.tile([P, HALF * PACK], BF16, name=f"z_hi{h}", align_bytes=64) for h in range(2)]
+        z_lo = [keep.tile([P, HALF * PACK], BF16, name=f"z_lo{h}", align_bytes=64) for h in range(2)]
         cols = [slice(h * HALF, (h + 1) * HALF) for h in range(2)]
         acc = [[psum.tile([P, HALF], F32, name=f"acc{h}_{b}") for b in range(N // P)] for h in range(2)]
+        sums = [[keep.tile([P, HALF], F32, name=f"sums{h}_{b}") for b in range(N // P)] for h in range(2)]
 
-        def look_up(t):
-            for offsets, val in ((list_a, val_a), (list_b, val_b)):
-                picked = ring.tile([P, J], U8, name="picked")
-                nc.vector.tensor_copy(picked[:], table[t][:].indirect(offsets[:]))
-                nc.scalar.copy(val[:, t, :], picked[:].bitcast(FP8))
+        def look_up(t, offsets):
+            picked = ring.tile([P, J], U8, name="picked")
+            nc.vector.tensor_copy(picked[:], table[t][:].indirect(offsets[:]))
+            return picked[:].bitcast(FP8)
 
-        def lower(t):
-            nc.vector.tensor_tensor(low[:, t, :], val_a[:, t, :], val_b[:, t, :], ALU.min)
-            for h in range(2):
-                nc.scalar.activation(out=z_lo[h][:, t :: PACK], in_=low[:, t, cols[h]], func=COPY, scale=step_lo[:, t : t + 1])
+        def look_up_pair(t):
+            nc.scalar.copy(val_a[:, t, :], look_up(t, list_a))
+            nc.scalar.copy(val_b[:, t, :], look_up(t, list_b))
 
-        def upper(h, slots):
-            nc.vector.tensor_tensor(high[h][:, slots, :], val_a[:, slots, cols[h]], val_b[:, slots, cols[h]], ALU.max)
+        def lower(slots, span):
+            nc.vector.tensor_tensor(low[:, slots, span], val_a[:, slots, span], val_b[:, slots, span], ALU.min)
+
+        def scale_lower(t, h):
+            nc.scalar.activation(out=z_lo[h][:, t::PACK], in_=low[:, t, cols[h]], func=COPY, scale=step_lo[:, t : t + 1])
+
+        def upper(h, slots, part):
+            span = slice(h * HALF + part.start, h * HALF + part.stop)
+            nc.vector.tensor_tensor(high[h][:, slots, part], val_a[:, slots, span], val_b[:, slots, span], ALU.max)
 
         def scale_upper(h):
             nc.vector.tensor_tensor(
                 z_hi[h][:].rearrange("p (c i t) -> p c t i", i=LINE, t=PACK),
-                high[h].rearrange("p t (c i) -> p c t i", i=LINE),
+                high[h][:].rearrange("p t (c i) -> p c t i", i=LINE),
                 step_hi[:].rearrange("p (a t b) -> p a t b", a=1, b=1).to_broadcast([P, HALF // LINE, PACK, LINE]),
                 ALU.mult,
             )
 
-        def product(h, z, name, weights, first):
-            codes = keep.tile([P, HALF], U32, name=f"codes_{name}{h}", align_bytes=64)
-            plane = keep.tile([P, HALF], U8, name=f"plane_{name}{h}", align_bytes=64)
-            nc.vector.quantize_mx(out=codes[:].bitcast(FP8X4), scales=plane[:], in_=z)
-            for b in range(N // P):
-                lhs, lhs_plane = weights(b)
-                nc.tensor.matmul_mx(
-                    out=acc[h][b][:], lhsT=lhs, lhsT_scale=lhs_plane, rhs=codes[:].bitcast(FP8X4), rhs_scale=plane[:], start=first, stop=not first
-                )
+        def quantise(z, name):
+            codes = keep.tile([P, HALF], U32, name=f"codes_{name}", align_bytes=64)
+            plane = keep.tile([P, HALF], U8, name=f"plane_{name}", align_bytes=64)
+            nc.vector.quantize_mx(out=codes[:].bitcast(FP8X4), scales=plane[:], in_=z[:])
+            return codes[:].bitcast(FP8X4), plane[:]
 
-        def w_upper(b):
-            return w_codes[:, b * P : (b + 1) * P].bitcast(FP8X4), w_plane[:, b * P : (b + 1) * P]
+        def lower_pass(h, b, moving):
+            nc.tensor.matmul_mx(
+                out=acc[h][b][:],
+                lhsT=w2_codes[:, 2 * b * P : 2 * (b + 1) * P].bitcast(FP4X4),
+                lhsT_scale=w_plane[:, N + b * P : N + (b + 1) * P],
+                rhs=moving[0],
+                rhs_scale=moving[1],
+                start=True,
+                stop=False,
+            )
 
-        def w_lower(b):
-            return w2_codes[:, 2 * b * P : 2 * (b + 1) * P].bitcast(FP4X4), w_plane[:, N + b * P : N + (b + 1) * P]
+        def upper_pass(h, b, moving):
+            nc.tensor.matmul_mx(
+                out=acc[h][b][:],
+                lhsT=w_codes[:, b * P : (b + 1) * P].bitcast(FP8X4),
+                lhsT_scale=w_plane[:, b * P : (b + 1) * P],
+                rhs=moving[0],
+                rhs_scale=moving[1],
+                start=False,
+                stop=True,
+            )
 
-        def put(h, copy):
-            sums = [keep.tile([P, HALF], F32, name=f"sums{h}_{b}") for b in range(N // P)]
-            for b in range(N // P):
-                copy(sums[b][:], acc[h][b][:])
-            for b in range(N // P):
-                nc.scalar.activation(
-                    out=pages[b][:].indirect(list_out[:, h * HALF // 16 : (h + 1) * HALF // 16]),
-                    in_=sums[b][:],
-                    func=COPY,
-                    scale=gain[:, b : b + 1],
-                )
+        def put(h, b):
+            nc.scalar.activation(
+                out=pages[b][:].indirect(list_out[:, h * HALF // 16 : (h + 1) * HALF // 16]),
+                in_=sums[h][b][:],
+                func=COPY,
+                scale=gain[:, b : b + 1],
+            )
 
-        look_up(0)
-        look_up(1)
-        lower(0)
-        look_up(2)
-        lower(1)
-        look_up(3)
-        lower(2)
-        upper(0, slice(0, PACK - 1))
-        upper(0, slice(PACK - 1, PACK))
-        lower(3)
+        last = PACK - 1
+        whole = slice(0, HALF)
+        look_up_pair(0)
+        for t in range(1, last):
+            look_up_pair(t)
+            lower(slice(t - 1, t), slice(0, J))
+            scale_lower(t - 1, 0)
+            scale_lower(t - 1, 1)
+        nc.scalar.copy(val_a[:, last, :], look_up(last, list_a))
+        last_b = look_up(last, list_b)
+        lower(slice(last - 1, last), cols[0])
+        scale_lower(last - 1, 0)
+        nc.vector.tensor_copy(val_b[:, last, :], last_b)
+        upper(0, slice(0, last), whole)
+        lower(slice(last, PACK), cols[0])
+        scale_lower(last, 0)
+        upper(0, slice(last, PACK), whole)
+        lower(slice(last - 1, PACK), cols[1])
+        scale_lower(last - 1, 1)
+        scale_lower(last, 1)
         scale_upper(0)
-        upper(1, slice(2, PACK))
-        product(0, z_hi[0][:], "hi", w_upper, True)
-        product(0, z_lo[0], "lo", w_lower, False)
-        upper(1, slice(0, 2))
-        product(1, z_lo[1], "lo", w_lower, True)
+        lo0 = quantise(z_lo[0], "lo0")
+        for b in range(N // P):
+            lower_pass(0, b, lo0)
+        hi0 = quantise(z_hi[0], "hi0")
+        for b in range(N // P):
+            upper_pass(0, b, hi0)
+        for b in range(N // P):
+            nc.scalar.copy(sums[0][b][:], acc[0][b][:])
+        for b in range(N // P):
+            put(0, b)
+        upper(1, slice(0, PACK), slice(0, HALF // 2))
+        upper(1, slice(0, PACK), slice(HALF // 2, HALF))
+        lo1 = quantise(z_lo[1], "lo1")
+        for b in range(N // P):
+            lower_pass(1, b, lo1)
         scale_upper(1)
-        put(0, nc.scalar.copy)
-        product(1, z_hi[1][:], "hi", w_upper, False)
-        put(1, nc.vector.tensor_copy)
+        hi1 = quantise(z_hi[1], "hi1")
+        for b in range(N // P):
+            upper_pass(1, b, hi1)
+            nc.vector.tensor_copy(sums[1][b][:], acc[1][b][:])
+            put(1, b)
         nc.sync.dma_start(out=out[0:P, :], in_=pages[0][:])
         nc.scalar.dma_start(out=out[P : 2 * P, :], in_=pages[1][:])

from contextlib import ExitStack

import concourse.mybir as mybir

K, V, J, N, E = 512, 1024, 256, 256, 512
FLOPS = 2 * 2 * K * N * J

F32 = mybir.dt.float32
BF16 = mybir.dt.bfloat16
I32 = mybir.dt.int32
U32 = mybir.dt.uint32
U16 = mybir.dt.uint16
U8 = mybir.dt.uint8
FP8 = mybir.dt.float8_e4m3fn
FP8X4 = mybir.dt.float8_e4m3fn_x4
FP4X4 = mybir.dt.float4_e2m1fn_x4
ALU = mybir.AluOpType
COPY = mybir.ActivationFunctionType.Copy

P = 128
PACK = 4
HALF = J // 2
LINE = 4


def tile_list_sortedpair_kernel(tc, ca, sa, sb, w_words, w_scales, w2_words, w2_scales, so, offs, offs2, offs3, out):
    nc = tc.nc
    with ExitStack() as ctx:
        keep = ctx.enter_context(tc.tile_pool(name="keep", bufs=1))
        ring = ctx.enter_context(tc.tile_pool(name="ring", bufs=3))
        psum = ctx.enter_context(tc.psum_pool(name="psum", bufs=1))

        table = [keep.tile([P, V], U8, name=f"table{t}") for t in range(PACK)]
        list_a = keep.tile([P, J // 16], U16, name="list_a")
        list_b = keep.tile([P, J // 16], U16, name="list_b")
        list_out = keep.tile([P, J // 16], U16, name="list_out")
        step_hi = keep.tile([P, PACK], F32, name="step_hi")
        step_lo = keep.tile([P, PACK], F32, name="step_lo")
        gain = keep.tile([P, N // P], F32, name="gain")
        w_codes = keep.tile([P, N], U32, name="w_codes", align_bytes=64)
        w2_codes = keep.tile([P, 2 * N], U8, name="w2_codes", align_bytes=64)
        w_plane = keep.tile([P, 2 * N], U8, name="w_plane", align_bytes=64)
        pages = [keep.tile([P, E], F32, name=f"page{b}") for b in range(N // P)]

        nc.vector.memset(w_plane[:].bitcast(I32), 0)
        for page in pages:
            nc.gpsimd.memset(page[:], 0.0)

        rows = ca.rearrange("(p t) v -> p t v", t=PACK)
        nc.sync.dma_start(out=table[0][:], in_=rows[:, 0, :])
        nc.sync.dma_start(list_a[:], offs)
        nc.sync.dma_start(list_b[:], offs2)
        for t in range(1, PACK):
            nc.sync.dma_start(out=table[t][:], in_=rows[:, t, :])
        nc.sync.dma_start(out=step_lo[:], in_=sb.rearrange("(p t) o -> p (t o)", t=PACK))
        nc.sync.dma_start(out=step_hi[:], in_=sa.rearrange("(p t) o -> p (t o)", t=PACK))
        nc.sync.dma_start(out=w_codes[:].bitcast(I32), in_=w_words[0].rearrange("p n t -> p (n t)").bitcast(I32))
        nc.sync.dma_start(out=w2_codes[:].bitcast(I32), in_=w2_words[0].bitcast(I32))
        for q in range(4):
            nc.sync.dma_start(out=w_plane[32 * q : 32 * q + 4, 0:N].bitcast(I32), in_=w_scales[0, 4 * q : 4 * q + 4, :].bitcast(I32))
            nc.sync.dma_start(out=w_plane[32 * q : 32 * q + 4, N : 2 * N].bitcast(I32), in_=w2_scales[0, 4 * q : 4 * q + 4, :].bitcast(I32))
        nc.sync.dma_start(list_out[:], offs3)
        with nc.allow_non_contiguous_dma(reason="one float32 a partition for each block of 128 output features"):
            nc.sync.dma_start(out=gain[:], in_=so.rearrange("(b p) o -> p (b o)", p=P))

        val_a = keep.tile([P, PACK, J], F32, name="val_a")
        val_b = keep.tile([P, PACK, J], F32, name="val_b")
        low = keep.tile([P, PACK, J], F32, name="low")
        high = [keep.tile([P, PACK, HALF], F32, name=f"high{h}") for h in range(2)]
        z_hi = [keep.tile([P, HALF * PACK], BF16, name=f"z_hi{h}", align_bytes=64) for h in range(2)]
        z_lo = [keep.tile([P, HALF * PACK], BF16, name=f"z_lo{h}", align_bytes=64) for h in range(2)]
        cols = [slice(h * HALF, (h + 1) * HALF) for h in range(2)]
        acc = [[psum.tile([P, HALF], F32, name=f"acc{h}_{b}") for b in range(N // P)] for h in range(2)]
        sums = [[keep.tile([P, HALF], F32, name=f"sums{h}_{b}") for b in range(N // P)] for h in range(2)]

        def look_up(t, offsets):
            picked = ring.tile([P, J], U8, name="picked")
            nc.vector.tensor_copy(picked[:], table[t][:].indirect(offsets[:]))
            return picked[:].bitcast(FP8)

        def look_up_pair(t):
            nc.scalar.copy(val_a[:, t, :], look_up(t, list_a))
            nc.scalar.copy(val_b[:, t, :], look_up(t, list_b))

        def lower(slots, span):
            nc.vector.tensor_tensor(low[:, slots, span], val_a[:, slots, span], val_b[:, slots, span], ALU.min)

        def scale_lower(t, h):
            nc.scalar.activation(out=z_lo[h][:, t::PACK], in_=low[:, t, cols[h]], func=COPY, scale=step_lo[:, t : t + 1])

        def upper(h, slots, part):
            span = slice(h * HALF + part.start, h * HALF + part.stop)
            nc.vector.tensor_tensor(high[h][:, slots, part], val_a[:, slots, span], val_b[:, slots, span], ALU.max)

        def scale_upper(h):
            nc.vector.tensor_tensor(
                z_hi[h][:].rearrange("p (c i t) -> p c t i", i=LINE, t=PACK),
                high[h][:].rearrange("p t (c i) -> p c t i", i=LINE),
                step_hi[:].rearrange("p (a t b) -> p a t b", a=1, b=1).to_broadcast([P, HALF // LINE, PACK, LINE]),
                ALU.mult,
            )

        def quantise(z, name):
            codes = keep.tile([P, HALF], U32, name=f"codes_{name}", align_bytes=64)
            plane = keep.tile([P, HALF], U8, name=f"plane_{name}", align_bytes=64)
            nc.vector.quantize_mx(out=codes[:].bitcast(FP8X4), scales=plane[:], in_=z[:])
            return codes[:].bitcast(FP8X4), plane[:]

        def lower_pass(h, b, moving):
            nc.tensor.matmul_mx(
                out=acc[h][b][:],
                lhsT=w2_codes[:, 2 * b * P : 2 * (b + 1) * P].bitcast(FP4X4),
                lhsT_scale=w_plane[:, N + b * P : N + (b + 1) * P],
                rhs=moving[0],
                rhs_scale=moving[1],
                start=True,
                stop=False,
            )

        def upper_pass(h, b, moving):
            nc.tensor.matmul_mx(
                out=acc[h][b][:],
                lhsT=w_codes[:, b * P : (b + 1) * P].bitcast(FP8X4),
                lhsT_scale=w_plane[:, b * P : (b + 1) * P],
                rhs=moving[0],
                rhs_scale=moving[1],
                start=False,
                stop=True,
            )

        def put(h, b):
            nc.scalar.activation(
                out=pages[b][:].indirect(list_out[:, h * HALF // 16 : (h + 1) * HALF // 16]),
                in_=sums[h][b][:],
                func=COPY,
                scale=gain[:, b : b + 1],
            )

        last = PACK - 1
        whole = slice(0, HALF)
        look_up_pair(0)
        for t in range(1, last):
            look_up_pair(t)
            lower(slice(t - 1, t), slice(0, J))
            scale_lower(t - 1, 0)
            scale_lower(t - 1, 1)
        nc.scalar.copy(val_a[:, last, :], look_up(last, list_a))
        last_b = look_up(last, list_b)
        lower(slice(last - 1, last), cols[0])
        scale_lower(last - 1, 0)
        nc.vector.tensor_copy(val_b[:, last, :], last_b)
        upper(0, slice(0, last), whole)
        lower(slice(last, PACK), cols[0])
        scale_lower(last, 0)
        upper(0, slice(last, PACK), whole)
        lower(slice(last - 1, PACK), cols[1])
        scale_lower(last - 1, 1)
        scale_lower(last, 1)
        scale_upper(0)
        lo0 = quantise(z_lo[0], "lo0")
        for b in range(N // P):
            lower_pass(0, b, lo0)
        hi0 = quantise(z_hi[0], "hi0")
        for b in range(N // P):
            upper_pass(0, b, hi0)
        for b in range(N // P):
            nc.scalar.copy(sums[0][b][:], acc[0][b][:])
        for b in range(N // P):
            put(0, b)
        upper(1, slice(0, PACK), slice(0, HALF // 2))
        upper(1, slice(0, PACK), slice(HALF // 2, HALF))
        lo1 = quantise(z_lo[1], "lo1")
        for b in range(N // P):
            lower_pass(1, b, lo1)
        scale_upper(1)
        hi1 = quantise(z_hi[1], "hi1")
        for b in range(N // P):
            upper_pass(1, b, hi1)
            nc.vector.tensor_copy(sums[1][b][:], acc[1][b][:])
            put(1, b)
        nc.sync.dma_start(out=out[0:P, :], in_=pages[0][:])
        nc.scalar.dma_start(out=out[P : 2 * P, :], in_=pages[1][:])
